import numpy as np, ml_dtypes
CORES = [32,40,48,56,64,72,80,88,96,104,112,120]
N = 12
TK = 256
def setup_inputs(rng):
    return {"x": rng.standard_normal((N, 128, N * TK), dtype=np.float32).astype(ml_dtypes.bfloat16), "t": rng.standard_normal((N, 128, N * TK), dtype=np.float32).astype(ml_dtypes.bfloat16), "f1": (rng.standard_normal((N, 128, 128), dtype=np.float32) / 11).astype(ml_dtypes.bfloat16), "f2": (rng.standard_normal((N, 128, 128), dtype=np.float32) / 11).astype(ml_dtypes.bfloat16)}
def setup_inputs_big(rng):
    d = setup_inputs(rng)
    for k in ("x", "t", "f1", "f2"): d[k] = (d[k].astype(np.float32) * 1024.0).astype(d[k].dtype)
    return d
def setup_inputs_small(rng):
    d = setup_inputs(rng)
    for k in ("x", "t", "f1", "f2"): d[k] = (d[k].astype(np.float32) * (1 / 1024.0)).astype(d[k].dtype)
    return d
def reference(x, t, f1, f2):
    X, T, F1, F2 = x.astype(np.float64), t.astype(np.float64), f1.astype(np.float64), f2.astype(np.float64)
    y = np.zeros((N, 128, N * TK))
    for j in range(N):
        u = (F1[j].T @ X[j]) * T[j]
        for r in range(N):
            y[r][:, TK * j:TK * j + TK] = F2[r].T @ u[:, TK * r:TK * r + TK]
    return {"y": y.astype(ml_dtypes.bfloat16)}

@@ -1,0 +1,265 @@
+from concourse.bass import DstId, RemoteDMATransfer
+from concourse.mybir import AluOpType
+
+N = 12
+TK = 256
+W = N * TK
+NG = 6
+MAXP = 2
+BANKS = 8
+SLOTS = 4
+
+CALLS = [
+    [((("S", 1),), "far_plain", "lo"), ((("X", 1),), "near_owner", "hi")],
+    [((("S", 2),), None, "lo"), ((("X", 2),), "far_owner", "hi")],
+    [((("S", 3),), "far_plain", "lo"), ((("X", 3),), "near_owner", "hi")],
+    [((("S", 4),), None, "lo"), ((("X", 4),), "far_owner", "hi")],
+    [((("S", 5),), None, "lo"), ((("X", 5),), "far_owner", "hi")],
+    [((("X", 0),), "near_owner", "all")],
+]
+RECV = [(("O", 0),), (("S", 1), ("X", 1)), (("S", 2), ("X", 2)), (("S", 3), ("X", 3)), (("S", 4), ("X", 4)),
+        (("S", 5), ("X", 5)), (("X", 0),)]
+HELPER_ENGINES = 8
+HOLD = {}
+
+SCRATCH = {
+    "xs": ("sbuf", [128, W], "bfloat16"),
+    "ts": ("sbuf", [128, W], "bfloat16"),
+    "us": ("sbuf", [128, W], "bfloat16"),
+    "land": ("sbuf", [128, W], "bfloat16"),
+    "ysb": ("sbuf", [128, W], "bfloat16"),
+    "f1s": ("sbuf", [128, 128], "bfloat16"),
+    "f2s": ("sbuf", [128, 128], "bfloat16"),
+    "relay": ("sbuf", [128, SLOTS * TK], "bfloat16"),
+}
+for _b in range(BANKS):
+    SCRATCH["ps%d" % _b] = ("psum", [128, 512], "float32")
+
+SEMAPHORES = (["sf1", "sf2", "yd", "ls"]
+              + ["sx%d" % k for k in range(NG)] + ["st%d" % k for k in range(NG)] + ["go%d" % k for k in range(NG)]
+              + ["m1_%d" % k for k in range(NG)] + ["ud%d" % k for k in range(N)]
+              + ["m2_%d" % k for k in range(N)] + ["cp%d" % k for k in range(N)]
+              + ["ar%d" % k for k in range(N)] + ["rl%d" % k for k in range(SLOTS)])
+
+
+def _bits(mask):
+    return [e for e in range(mask.bit_length()) if (mask >> e) & 1]
+
+
+def _mask(engines):
+    m = 0
+    for e in engines:
+        m |= 1 << e
+    return m
+
+
+def _groups(T, topo):
+    cores = list(T.cores)
+    chips = [topo.chip(c) for c in cores]
+    groups, gid = [], {}
+    for i in range(len(cores)):
+        if i in gid:
+            continue
+        members = [i] + [j for j in range(i + 1, len(cores)) if topo.mates(chips[i], chips[j])]
+        for j in members:
+            gid[j] = len(groups)
+        groups.append(members)
+    return cores, chips, groups, gid
+
+
+def _who(r, kind, d, chips, groups, gid, topo):
+    return [j for j in groups[(gid[r] + d) % len(groups)]
+            if j != r and topo.same_plane(chips[r], chips[j]) == (kind == "S")][0]
+
+
+def _plan(r, cores, chips, groups, gid, topo):
+    me, ch = cores[r], chips[r]
+    mate = _who(r, "X", 0, chips, groups, gid, topo)
+    local = [c for c in range(topo.CHIPS * topo.CORES_PER_CHIP) if topo.chip(c) == ch and c != me]
+    owners = [c for c in local if topo.may_write(c, cores[mate])]
+    near = [c for c in local if topo.die(c) == topo.die(me)]
+    helper = {
+        "near_owner": [c for c in owners if c in near][0],
+        "far_owner": [c for c in owners if c not in near][0],
+        "near_plain": [c for c in near if c not in owners][0],
+        "far_plain": [c for c in local if c not in owners and c not in near][0],
+    }
+    sets = {"all": _bits(topo.mask(me, local[0])), "lo": _bits(topo.mask(me, cores[mate]))}
+    sets["hi"] = [e for e in sets["all"] if e not in sets["lo"]]
+    for name in ("lo", "hi"):
+        half = len(sets[name]) // 2
+        sets[name + "0"], sets[name + "1"] = sets[name][:half], sets[name][half:]
+    slots, landings, calls, seq = {}, {}, [], []
+    for call in CALLS:
+        transfers = []
+        for blocks, way, engines in call:
+            ranks = [_who(r, kind, d, chips, groups, gid, topo) for kind, d in blocks]
+            via = helper[way] if way else None
+            tr = {"dst": ranks, "via": via, "engines": sets[engines], "slot": slots.get(via, 0), "landing": landings.get(via, 0)}
+            slots[via] = tr["slot"] + len(ranks)
+            landings[via] = tr["landing"] + 1
+            transfers.append(tr)
+            seq.extend(ranks)
+        calls.append(transfers)
+    if all(len(tr["dst"]) == 1 for c in calls for tr in c):
+        place = {j: j for j in range(len(cores))}
+    else:
+        place = {j: k for k, j in enumerate(seq + [r])}
+    return calls, place
+
+
+def _forward(via, tr, cores, topo):
+    n = len(tr["dst"])
+    out = []
+    for k, j in enumerate(tr["dst"]):
+        engines = _bits(topo.mask(via, cores[j]))[:HELPER_ENGINES]
+        share = len(engines) // n
+        out.append(engines[k * share:(k + 1) * share])
+    return out
+
+
+def _helper(g, core, r, T, topo, cores, chips, groups, gid):
+    sent = 0
+    for call in _plan(r, cores, chips, groups, gid, topo)[0]:
+        for tr in call:
+            if tr["via"] != core:
+                continue
+            g.wait_ge(T.sem["rl%d" % tr["landing"]], len(tr["engines"]))
+            transfers = []
+            for k, (j, engines) in enumerate(zip(tr["dst"], _forward(core, tr, cores, topo))):
+                rid, pid, _se = topo.addr(cores[j])
+                s = tr["slot"] + k
+                transfers.append(RemoteDMATransfer(dst_ids=[DstId(rid=rid, pnc=pid)], dma_engine_mask=_mask(engines),
+                                                   remote_sem=T.sem["ar%d" % r], src=T.relay[:, s * TK:(s + 1) * TK],
+                                                   dst=T.land[:, r * TK:(r + 1) * TK]))
+                sent += len(engines)
+            g.remote_dma_fused(transfers, local_sem=T.sem.ls)
+    if sent:
+        g.wait_ge(T.sem.ls, sent)
+
+
+def _incoming(r, j, cores, chips, groups, gid, topo):
+    for call in _plan(j, cores, chips, groups, gid, topo)[0]:
+        for tr in call:
+            if r in tr["dst"]:
+                if tr["via"] is None:
+                    return len(tr["engines"])
+                return len(_forward(tr["via"], tr, cores, topo)[tr["dst"].index(r)])
+
+
+def rank_program(g, core, T, topo):
+    cores, chips, groups, gid = _groups(T, topo)
+    rank = T.rank_of(core)
+    if rank is None:
+        here = [r for r in range(len(cores)) if chips[r] == topo.chip(core)]
+        if here:
+            _helper(g, core, here[0], T, topo, cores, chips, groups, gid)
+        return
+
+    sem, te, ve = T.sem, g.tensor, g.vector
+    G = len(groups)
+    q = gid[rank]
+    mate = _who(rank, "X", 0, chips, groups, gid, topo)
+    calls, place = _plan(rank, cores, chips, groups, gid, topo)
+    order = [(q + d) % G for d in range(1, G)] + [q]
+
+    def cols(grp):
+        return groups[grp][0] * TK, (groups[grp][-1] + 1) * TK
+
+    def u_of(j, n=1):
+        return T.us[:, place[j] * TK:(place[j] + n) * TK]
+
+    pieces = []
+    for grp in order:
+        if len(pieces) > 1 and pieces[-1][-1] + 1 == grp and len(pieces[-1]) < MAXP:
+            pieces[-1].append(grp)
+        else:
+            pieces.append([grp])
+    piece_of = {grp: k for k, p in enumerate(pieces) for grp in p}
+    g.sync.dma_start(T.f1s[:], T.f1[:]).then_inc(sem.sf1, 16)
+    for k, p in enumerate(pieces):
+        a, b = cols(p[0])[0], cols(p[-1])[1]
+        if k in HOLD:
+            g.sync.wait_ge(sem["go%d" % k], 1)
+            g.scalar.wait_ge(sem["go%d" % k], 1)
+        g.sync.dma_start(T.xs[:, a:b], T.x[:, a:b]).then_inc(sem["sx%d" % k], 16)
+        g.scalar.dma_start(T.ts[:, a:b], T.t[:, a:b]).then_inc(sem["st%d" % k], 16)
+    g.scalar.dma_start(T.f2s[:], T.f2[:]).then_inc(sem.sf2, 16)
+
+    done = {}
+    te.wait_ge(sem.sf1, 16)
+    for i, grp in enumerate(order):
+        a, b = cols(grp)
+        te.wait_ge(sem["sx%d" % piece_of[grp]], 16)
+        te.matmul(T["ps%d" % i][:, 0:b - a], T.f1s[:], T.xs[:, a:b], start=True, stop=True).then_inc(sem["m1_%d" % i], 1)
+        ve.wait_ge(sem["m1_%d" % i], 1)
+        ve.wait_ge(sem["st%d" % piece_of[grp]], 16)
+        j0, j1 = groups[grp]
+        if grp == q:
+            parts = [[mate], [rank]]
+        elif place[j1] == place[j0] + 1:
+            parts = [[j0, j1]]
+        else:
+            parts = [[j0], [j1]]
+        for part in parts:
+            c0, c1 = part[0] * TK, (part[-1] + 1) * TK
+            for j in part:
+                done[j] = "ud%d" % part[0]
+            ve.tensor_tensor(out=u_of(part[0], len(part)), in0=T["ps%d" % i][:, c0 - a:c1 - a], in1=T.ts[:, c0:c1],
+                             op=AluOpType.mult).then_inc(sem[done[part[0]]], 1)
+
+    sent = 0
+    for i, call in enumerate(calls):
+        for name in sorted({done[j] for tr in call for j in tr["dst"]}):
+            g.wait_ge(sem[name], 1)
+        transfers = []
+        for tr in call:
+            n = len(tr["dst"])
+            if tr["via"] is None:
+                target, out, arrived = cores[tr["dst"][0]], T.land[:, rank * TK:(rank + 1) * TK], sem["ar%d" % rank]
+            else:
+                target, out = tr["via"], T.relay[:, tr["slot"] * TK:(tr["slot"] + n) * TK]
+                arrived = sem["rl%d" % tr["landing"]]
+            rid, pid, _se = topo.addr(target)
+            transfers.append(RemoteDMATransfer(dst_ids=[DstId(rid=rid, pnc=pid)], dma_engine_mask=_mask(tr["engines"]),
+                                               remote_sem=arrived, src=u_of(tr["dst"][0], n), dst=out))
+            sent += len(tr["engines"])
+        g.remote_dma_fused(transfers, local_sem=sem.ls)
+        for k in sorted(HOLD):
+            if HOLD[k] == i and k < len(pieces):
+                g.sem_inc(sem["go%d" % k], 1)
+
+    queues, stores = [g.sync, g.scalar], 0
+    copied = {}
+    te.wait_ge(sem.sf2, 16)
+    for k, entry in enumerate(RECV):
+        srcs = sorted(rank if kind == "O" else _who(rank, kind, -d, chips, groups, gid, topo) for kind, d in entry)
+        a, b = srcs[0] * TK, (srcs[-1] + 1) * TK
+        bank = (G + k) % BANKS
+        for j in srcs:
+            if j == rank:
+                te.wait_ge(sem[done[rank]], 1)
+            else:
+                te.wait_ge(sem["ar%d" % j], _incoming(rank, j, cores, chips, groups, gid, topo))
+        if k >= BANKS:
+            te.wait_ge(sem["cp%d" % (k - BANKS)], 1)
+        elif bank < G:
+            for name in sorted({done[j] for j in groups[order[bank]]}):
+                te.wait_ge(sem[name], 1)
+        te.matmul(T["ps%d" % bank][:, 0:b - a], T.f2s[:], u_of(rank) if srcs == [rank] else T.land[:, a:b],
+                  start=True, stop=True).then_inc(sem["m2_%d" % k], 1)
+        ve.wait_ge(sem["m2_%d" % k], 1)
+        ve.tensor_copy(T.ysb[:, a:b], T["ps%d" % bank][:, 0:b - a]).then_inc(sem["cp%d" % k], 1)
+        for j in srcs:
+            copied[j] = "cp%d" % k
+        members = groups[gid[srcs[0]]]
+        if all(j in copied for j in members):
+            a, b = cols(gid[srcs[0]])
+            qu = queues[stores % 2]
+            for name in sorted({copied[j] for j in members}):
+                qu.wait_ge(sem[name], 1)
+            qu.dma_start(T.y[:, a:b], T.ysb[:, a:b]).then_inc(sem.yd, 16)
+            stores += 1
+
+    g.wait_ge(sem.ls, sent)
+    g.wait_ge(sem.yd, 16 * stores)

@@ -4,23 +4,25 @@ from concourse.mybir import AluOpType
 N = 12
 TK = 256
 W = N * TK
-NG = 6
-MAXP = 2
 BANKS = 8
 SLOTS = 4
+NDMA = 8
 
 CALLS = [
-    [((("S", 1),), "far_plain", "lo"), ((("X", 1),), "near_owner", "hi")],
-    [((("S", 2),), None, "lo"), ((("X", 2),), "far_owner", "hi")],
-    [((("S", 3),), "far_plain", "lo"), ((("X", 3),), "near_owner", "hi")],
-    [((("S", 4),), None, "lo"), ((("X", 4),), "far_owner", "hi")],
-    [((("S", 5),), None, "lo"), ((("X", 5),), "far_owner", "hi")],
-    [((("X", 0),), "near_owner", "all")],
+    [(("X", 0), "near_owner", "all")],
+    [(("X", 1), "far_owner", "hi"), (("S", 1), None, "lo")],
+    [(("X", 2), "far_owner2", "hi"), (("S", 2), None, "lo")],
+    [(("X", 3), "near_owner", "hi"), (("S", 3), None, "lo")],
+    [(("X", 4), "far_owner", "hi"), (("S", 4), None, "lo")],
+    [(("X", 5), "far_owner2", "hi")],
+    [(("S", 5), None, "lo")],
 ]
-RECV = [(("O", 0),), (("S", 1), ("X", 1)), (("S", 2), ("X", 2)), (("S", 3), ("X", 3)), (("S", 4), ("X", 4)),
-        (("S", 5), ("X", 5)), (("X", 0),)]
-HELPER_ENGINES = 8
-HOLD = {}
+LOADS = [[("X", 0)], [("S", 1), ("X", 1), ("S", 2), ("X", 2)], [("S", 3), ("X", 3), ("S", 4), ("X", 4)],
+         [("S", 5), ("X", 5)], [("O", 0)]]
+UNITS = [[("X", 0)], [("S", 1), ("X", 1)], [("S", 2), ("X", 2)], [("S", 3), ("X", 3)], [("S", 4), ("X", 4)],
+         [("X", 5)], [("S", 5)], [("O", 0)]]
+RECV = [("O", 0), ("S", 1), ("S", 2), ("S", 3), ("S", 4), ("S", 5), ("X", 0), ("X", 1), ("X", 2), ("X", 3), ("X", 4), ("X", 5)]
+SPLIT = (4, 5)
 
 SCRATCH = {
     "xs": ("sbuf", [128, W], "bfloat16"),
@@ -36,8 +38,8 @@ for _b in range(BANKS):
     SCRATCH["ps%d" % _b] = ("psum", [128, 512], "float32")
 
 SEMAPHORES = (["sf1", "sf2", "yd", "ls"]
-              + ["sx%d" % k for k in range(NG)] + ["st%d" % k for k in range(NG)] + ["go%d" % k for k in range(NG)]
-              + ["m1_%d" % k for k in range(NG)] + ["ud%d" % k for k in range(N)]
+              + ["sx%d" % k for k in range(NDMA)] + ["st%d" % k for k in range(NDMA)]
+              + ["m1_%d" % k for k in range(N)] + ["ud%d" % k for k in range(N)]
               + ["m2_%d" % k for k in range(N)] + ["cp%d" % k for k in range(N)]
               + ["ar%d" % k for k in range(N)] + ["rl%d" % k for k in range(SLOTS)])
 
@@ -68,6 +70,8 @@ def _groups(T, topo):
 
 
 def _who(r, kind, d, chips, groups, gid, topo):
+    if kind == "O":
+        return r
     return [j for j in groups[(gid[r] + d) % len(groups)]
             if j != r and topo.same_plane(chips[r], chips[j]) == (kind == "S")][0]
 
@@ -81,70 +85,64 @@ def _plan(r, cores, chips, groups, gid, topo):
     helper = {
         "near_owner": [c for c in owners if c in near][0],
         "far_owner": [c for c in owners if c not in near][0],
-        "near_plain": [c for c in near if c not in owners][0],
-        "far_plain": [c for c in local if c not in owners and c not in near][0],
+        "far_owner2": [c for c in owners if c not in near][1],
     }
     sets = {"all": _bits(topo.mask(me, local[0])), "lo": _bits(topo.mask(me, cores[mate]))}
     sets["hi"] = [e for e in sets["all"] if e not in sets["lo"]]
-    for name in ("lo", "hi"):
-        half = len(sets[name]) // 2
-        sets[name + "0"], sets[name + "1"] = sets[name][:half], sets[name][half:]
-    slots, landings, calls, seq = {}, {}, [], []
+    slots, calls = {}, []
     for call in CALLS:
         transfers = []
-        for blocks, way, engines in call:
-            ranks = [_who(r, kind, d, chips, groups, gid, topo) for kind, d in blocks]
+        for (kind, d), way, engines in call:
             via = helper[way] if way else None
-            tr = {"dst": ranks, "via": via, "engines": sets[engines], "slot": slots.get(via, 0), "landing": landings.get(via, 0)}
-            slots[via] = tr["slot"] + len(ranks)
-            landings[via] = tr["landing"] + 1
+            tr = {"dst": _who(r, kind, d, chips, groups, gid, topo), "via": via, "engines": sets[engines],
+                  "slot": slots.get(via, 0), "fwd": None}
+            slots[via] = tr["slot"] + 1
             transfers.append(tr)
-            seq.extend(ranks)
+        for via in sorted({tr["via"] for tr in transfers if tr["via"] is not None}):
+            mine = [tr for tr in transfers if tr["via"] == via]
+            for k, tr in enumerate(mine):
+                engines = _bits(topo.mask(via, cores[tr["dst"]]))
+                share = len(engines) // len(mine)
+                tr["fwd"] = engines[k * share:(k + 1) * share]
         calls.append(transfers)
-    if all(len(tr["dst"]) == 1 for c in calls for tr in c):
-        place = {j: j for j in range(len(cores))}
-    else:
-        place = {j: k for k, j in enumerate(seq + [r])}
-    return calls, place
-
-
-def _forward(via, tr, cores, topo):
-    n = len(tr["dst"])
-    out = []
-    for k, j in enumerate(tr["dst"]):
-        engines = _bits(topo.mask(via, cores[j]))[:HELPER_ENGINES]
-        share = len(engines) // n
-        out.append(engines[k * share:(k + 1) * share])
-    return out
+    return calls
 
 
 def _helper(g, core, r, T, topo, cores, chips, groups, gid):
     sent = 0
-    for call in _plan(r, cores, chips, groups, gid, topo)[0]:
-        for tr in call:
-            if tr["via"] != core:
-                continue
-            g.wait_ge(T.sem["rl%d" % tr["landing"]], len(tr["engines"]))
-            transfers = []
-            for k, (j, engines) in enumerate(zip(tr["dst"], _forward(core, tr, cores, topo))):
-                rid, pid, _se = topo.addr(cores[j])
-                s = tr["slot"] + k
-                transfers.append(RemoteDMATransfer(dst_ids=[DstId(rid=rid, pnc=pid)], dma_engine_mask=_mask(engines),
-                                                   remote_sem=T.sem["ar%d" % r], src=T.relay[:, s * TK:(s + 1) * TK],
-                                                   dst=T.land[:, r * TK:(r + 1) * TK]))
-                sent += len(engines)
-            g.remote_dma_fused(transfers, local_sem=T.sem.ls)
+    for call in _plan(r, cores, chips, groups, gid, topo):
+        mine = [tr for tr in call if tr["via"] == core]
+        if not mine:
+            continue
+        transfers = []
+        for tr in mine:
+            g.wait_ge(T.sem["rl%d" % tr["slot"]], len(tr["engines"]))
+            rid, pid, _se = topo.addr(cores[tr["dst"]])
+            s = tr["slot"]
+            transfers.append(RemoteDMATransfer(dst_ids=[DstId(rid=rid, pnc=pid)], dma_engine_mask=_mask(tr["fwd"]),
+                                               remote_sem=T.sem["ar%d" % r], src=T.relay[:, s * TK:(s + 1) * TK],
+                                               dst=T.land[:, r * TK:(r + 1) * TK]))
+            sent += len(tr["fwd"])
+        g.remote_dma_fused(transfers, local_sem=T.sem.ls)
     if sent:
         g.wait_ge(T.sem.ls, sent)
 
 
 def _incoming(r, j, cores, chips, groups, gid, topo):
-    for call in _plan(j, cores, chips, groups, gid, topo)[0]:
+    for call in _plan(j, cores, chips, groups, gid, topo):
         for tr in call:
-            if r in tr["dst"]:
-                if tr["via"] is None:
-                    return len(tr["engines"])
-                return len(_forward(tr["via"], tr, cores, topo)[tr["dst"].index(r)])
+            if tr["dst"] == r:
+                return len(tr["engines"]) if tr["via"] is None else len(tr["fwd"])
+
+
+def _runs(blocks):
+    out = []
+    for j in sorted(blocks):
+        if out and out[-1][-1] + 1 == j:
+            out[-1].append(j)
+        else:
+            out.append([j])
+    return out
 
 
 def rank_program(g, core, T, topo):
@@ -157,106 +155,86 @@ def rank_program(g, core, T, topo):
         return
 
     sem, te, ve = T.sem, g.tensor, g.vector
-    G = len(groups)
-    q = gid[rank]
-    mate = _who(rank, "X", 0, chips, groups, gid, topo)
-    calls, place = _plan(rank, cores, chips, groups, gid, topo)
-    order = [(q + d) % G for d in range(1, G)] + [q]
+    calls = _plan(rank, cores, chips, groups, gid, topo)
 
-    def cols(grp):
-        return groups[grp][0] * TK, (groups[grp][-1] + 1) * TK
+    def to(kind, d):
+        return _who(rank, kind, d, chips, groups, gid, topo)
 
-    def u_of(j, n=1):
-        return T.us[:, place[j] * TK:(place[j] + n) * TK]
-
-    pieces = []
-    for grp in order:
-        if len(pieces) > 1 and pieces[-1][-1] + 1 == grp and len(pieces[-1]) < MAXP:
-            pieces[-1].append(grp)
-        else:
-            pieces.append([grp])
-    piece_of = {grp: k for k, p in enumerate(pieces) for grp in p}
-    g.sync.dma_start(T.f1s[:], T.f1[:]).then_inc(sem.sf1, 16)
-    for k, p in enumerate(pieces):
-        a, b = cols(p[0])[0], cols(p[-1])[1]
-        if k in HOLD:
-            g.sync.wait_ge(sem["go%d" % k], 1)
-            g.scalar.wait_ge(sem["go%d" % k], 1)
-        g.sync.dma_start(T.xs[:, a:b], T.x[:, a:b]).then_inc(sem["sx%d" % k], 16)
-        g.scalar.dma_start(T.ts[:, a:b], T.t[:, a:b]).then_inc(sem["st%d" % k], 16)
-    g.scalar.dma_start(T.f2s[:], T.f2[:]).then_inc(sem.sf2, 16)
+    dma_of, n = {}, 0
+    g.scalar.dma_start(T.f1s[:], T.f1[:]).then_inc(sem.sf1, 16)
+    for k, piece in enumerate(LOADS):
+        if k == len(LOADS) - 1:
+            g.scalar.dma_start(T.f2s[:], T.f2[:]).then_inc(sem.sf2, 16)
+        for run in _runs([to(kind, d) for kind, d in piece]):
+            a, b = run[0] * TK, (run[-1] + 1) * TK
+            g.sync.dma_start(T.xs[:, a:b], T.x[:, a:b]).then_inc(sem["sx%d" % n], 16)
+            g.scalar.dma_start(T.ts[:, a:b], T.t[:, a:b]).then_inc(sem["st%d" % n], 16)
+            for j in run:
+                dma_of[j] = n
+            n += 1
 
     done = {}
+    reader = {}
     te.wait_ge(sem.sf1, 16)
-    for i, grp in enumerate(order):
-        a, b = cols(grp)
-        te.wait_ge(sem["sx%d" % piece_of[grp]], 16)
-        te.matmul(T["ps%d" % i][:, 0:b - a], T.f1s[:], T.xs[:, a:b], start=True, stop=True).then_inc(sem["m1_%d" % i], 1)
+    for i, unit in enumerate(UNITS):
+        blocks = sorted(to(kind, d) for kind, d in unit)
+        a, b = blocks[0] * TK, (blocks[-1] + 1) * TK
+        bank = i % BANKS
+        if bank in reader:
+            te.wait_ge(sem[reader[bank]], 1)
+        for k in sorted({dma_of[j] for j in blocks}):
+            te.wait_ge(sem["sx%d" % k], 16)
+        te.matmul(T["ps%d" % bank][:, 0:b - a], T.f1s[:], T.xs[:, a:b], start=True, stop=True).then_inc(sem["m1_%d" % i], 1)
         ve.wait_ge(sem["m1_%d" % i], 1)
-        ve.wait_ge(sem["st%d" % piece_of[grp]], 16)
-        j0, j1 = groups[grp]
-        if grp == q:
-            parts = [[mate], [rank]]
-        elif place[j1] == place[j0] + 1:
-            parts = [[j0, j1]]
-        else:
-            parts = [[j0], [j1]]
-        for part in parts:
-            c0, c1 = part[0] * TK, (part[-1] + 1) * TK
-            for j in part:
-                done[j] = "ud%d" % part[0]
-            ve.tensor_tensor(out=u_of(part[0], len(part)), in0=T["ps%d" % i][:, c0 - a:c1 - a], in1=T.ts[:, c0:c1],
-                             op=AluOpType.mult).then_inc(sem[done[part[0]]], 1)
+        for k in sorted({dma_of[j] for j in blocks}):
+            ve.wait_ge(sem["st%d" % k], 16)
+        ve.tensor_tensor(out=T.us[:, a:b], in0=T["ps%d" % bank][:, 0:b - a], in1=T.ts[:, a:b],
+                         op=AluOpType.mult).then_inc(sem["ud%d" % i], 1)
+        reader[bank] = "ud%d" % i
+        for j in blocks:
+            done[j] = "ud%d" % i
 
     sent = 0
-    for i, call in enumerate(calls):
-        for name in sorted({done[j] for tr in call for j in tr["dst"]}):
+    for call in calls:
+        for name in sorted({done[tr["dst"]] for tr in call}):
             g.wait_ge(sem[name], 1)
         transfers = []
         for tr in call:
-            n = len(tr["dst"])
+            j = tr["dst"]
             if tr["via"] is None:
-                target, out, arrived = cores[tr["dst"][0]], T.land[:, rank * TK:(rank + 1) * TK], sem["ar%d" % rank]
+                target, out, arrived = cores[j], T.land[:, rank * TK:(rank + 1) * TK], sem["ar%d" % rank]
             else:
-                target, out = tr["via"], T.relay[:, tr["slot"] * TK:(tr["slot"] + n) * TK]
-                arrived = sem["rl%d" % tr["landing"]]
+                target, out = tr["via"], T.relay[:, tr["slot"] * TK:(tr["slot"] + 1) * TK]
+                arrived = sem["rl%d" % tr["slot"]]
             rid, pid, _se = topo.addr(target)
             transfers.append(RemoteDMATransfer(dst_ids=[DstId(rid=rid, pnc=pid)], dma_engine_mask=_mask(tr["engines"]),
-                                               remote_sem=arrived, src=u_of(tr["dst"][0], n), dst=out))
+                                               remote_sem=arrived, src=T.us[:, j * TK:(j + 1) * TK], dst=out))
             sent += len(tr["engines"])
         g.remote_dma_fused(transfers, local_sem=sem.ls)
-        for k in sorted(HOLD):
-            if HOLD[k] == i and k < len(pieces):
-                g.sem_inc(sem["go%d" % k], 1)
 
     queues, stores = [g.sync, g.scalar], 0
     copied = {}
     te.wait_ge(sem.sf2, 16)
-    for k, entry in enumerate(RECV):
-        srcs = sorted(rank if kind == "O" else _who(rank, kind, -d, chips, groups, gid, topo) for kind, d in entry)
-        a, b = srcs[0] * TK, (srcs[-1] + 1) * TK
-        bank = (G + k) % BANKS
-        for j in srcs:
-            if j == rank:
-                te.wait_ge(sem[done[rank]], 1)
-            else:
-                te.wait_ge(sem["ar%d" % j], _incoming(rank, j, cores, chips, groups, gid, topo))
-        if k >= BANKS:
-            te.wait_ge(sem["cp%d" % (k - BANKS)], 1)
-        elif bank < G:
-            for name in sorted({done[j] for j in groups[order[bank]]}):
-                te.wait_ge(sem[name], 1)
-        te.matmul(T["ps%d" % bank][:, 0:b - a], T.f2s[:], u_of(rank) if srcs == [rank] else T.land[:, a:b],
+    for k, (kind, d) in enumerate(RECV):
+        j = to(kind, -d)
+        a, b = j * TK, (j + 1) * TK
+        bank = (len(UNITS) + k) % BANKS
+        if j == rank:
+            te.wait_ge(sem[done[rank]], 1)
+        else:
+            te.wait_ge(sem["ar%d" % j], _incoming(rank, j, cores, chips, groups, gid, topo))
+        te.wait_ge(sem[reader[bank]], 1)
+        te.matmul(T["ps%d" % bank][:, 0:TK], T.f2s[:], T.us[:, a:b] if j == rank else T.land[:, a:b],
                   start=True, stop=True).then_inc(sem["m2_%d" % k], 1)
         ve.wait_ge(sem["m2_%d" % k], 1)
-        ve.tensor_copy(T.ysb[:, a:b], T["ps%d" % bank][:, 0:b - a]).then_inc(sem["cp%d" % k], 1)
-        for j in srcs:
-            copied[j] = "cp%d" % k
-        members = groups[gid[srcs[0]]]
-        if all(j in copied for j in members):
-            a, b = cols(gid[srcs[0]])
+        ve.tensor_copy(T.ysb[:, a:b], T["ps%d" % bank][:, 0:TK]).then_inc(sem["cp%d" % k], 1)
+        reader[bank] = "cp%d" % k
+        copied[j] = "cp%d" % k
+        members = [j] if d in SPLIT else groups[gid[j]]
+        if all(m in copied for m in members):
+            a, b = members[0] * TK, (members[-1] + 1) * TK
             qu = queues[stores % 2]
-            for name in sorted({copied[j] for j in members}):
+            for name in sorted({copied[m] for m in members}):
                 qu.wait_ge(sem[name], 1)
             qu.dma_start(T.y[:, a:b], T.ysb[:, a:b]).then_inc(sem.yd, 16)
             stores += 1

from concourse.bass import DstId, RemoteDMATransfer
from concourse.mybir import AluOpType

N = 12
TK = 256
W = N * TK
BANKS = 8
SLOTS = 4
NDMA = 8

CALLS = [
    [(("X", 0), "near_owner", "all")],
    [(("X", 1), "far_owner", "hi"), (("S", 1), None, "lo")],
    [(("X", 2), "far_owner2", "hi"), (("S", 2), None, "lo")],
    [(("X", 3), "near_owner", "hi"), (("S", 3), None, "lo")],
    [(("X", 4), "far_owner", "hi"), (("S", 4), None, "lo")],
    [(("X", 5), "far_owner2", "hi")],
    [(("S", 5), None, "lo")],
]
LOADS = [[("X", 0)], [("S", 1), ("X", 1), ("S", 2), ("X", 2)], [("S", 3), ("X", 3), ("S", 4), ("X", 4)],
         [("S", 5), ("X", 5)], [("O", 0)]]
UNITS = [[("X", 0)], [("S", 1), ("X", 1)], [("S", 2), ("X", 2)], [("S", 3), ("X", 3)], [("S", 4), ("X", 4)],
         [("X", 5)], [("S", 5)], [("O", 0)]]
RECV = [("O", 0), ("S", 1), ("S", 2), ("S", 3), ("S", 4), ("S", 5), ("X", 0), ("X", 1), ("X", 2), ("X", 3), ("X", 4), ("X", 5)]
SPLIT = (4, 5)

SCRATCH = {
    "xs": ("sbuf", [128, W], "bfloat16"),
    "ts": ("sbuf", [128, W], "bfloat16"),
    "us": ("sbuf", [128, W], "bfloat16"),
    "land": ("sbuf", [128, W], "bfloat16"),
    "ysb": ("sbuf", [128, W], "bfloat16"),
    "f1s": ("sbuf", [128, 128], "bfloat16"),
    "f2s": ("sbuf", [128, 128], "bfloat16"),
    "relay": ("sbuf", [128, SLOTS * TK], "bfloat16"),
}
for _b in range(BANKS):
    SCRATCH["ps%d" % _b] = ("psum", [128, 512], "float32")

SEMAPHORES = (["sf1", "sf2", "yd", "ls"]
              + ["sx%d" % k for k in range(NDMA)] + ["st%d" % k for k in range(NDMA)]
              + ["m1_%d" % k for k in range(N)] + ["ud%d" % k for k in range(N)]
              + ["m2_%d" % k for k in range(N)] + ["cp%d" % k for k in range(N)]
              + ["ar%d" % k for k in range(N)] + ["rl%d" % k for k in range(SLOTS)])


def _bits(mask):
    return [e for e in range(mask.bit_length()) if (mask >> e) & 1]


def _mask(engines):
    m = 0
    for e in engines:
        m |= 1 << e
    return m


def _groups(T, topo):
    cores = list(T.cores)
    chips = [topo.chip(c) for c in cores]
    groups, gid = [], {}
    for i in range(len(cores)):
        if i in gid:
            continue
        members = [i] + [j for j in range(i + 1, len(cores)) if topo.mates(chips[i], chips[j])]
        for j in members:
            gid[j] = len(groups)
        groups.append(members)
    return cores, chips, groups, gid


def _who(r, kind, d, chips, groups, gid, topo):
    if kind == "O":
        return r
    return [j for j in groups[(gid[r] + d) % len(groups)]
            if j != r and topo.same_plane(chips[r], chips[j]) == (kind == "S")][0]


def _plan(r, cores, chips, groups, gid, topo):
    me, ch = cores[r], chips[r]
    mate = _who(r, "X", 0, chips, groups, gid, topo)
    local = [c for c in range(topo.CHIPS * topo.CORES_PER_CHIP) if topo.chip(c) == ch and c != me]
    owners = [c for c in local if topo.may_write(c, cores[mate])]
    near = [c for c in local if topo.die(c) == topo.die(me)]
    helper = {
        "near_owner": [c for c in owners if c in near][0],
        "far_owner": [c for c in owners if c not in near][0],
        "far_owner2": [c for c in owners if c not in near][1],
    }
    sets = {"all": _bits(topo.mask(me, local[0])), "lo": _bits(topo.mask(me, cores[mate]))}
    sets["hi"] = [e for e in sets["all"] if e not in sets["lo"]]
    slots, calls = {}, []
    for call in CALLS:
        transfers = []
        for (kind, d), way, engines in call:
            via = helper[way] if way else None
            tr = {"dst": _who(r, kind, d, chips, groups, gid, topo), "via": via, "engines": sets[engines],
                  "slot": slots.get(via, 0), "fwd": None}
            slots[via] = tr["slot"] + 1
            transfers.append(tr)
        for via in sorted({tr["via"] for tr in transfers if tr["via"] is not None}):
            mine = [tr for tr in transfers if tr["via"] == via]
            for k, tr in enumerate(mine):
                engines = _bits(topo.mask(via, cores[tr["dst"]]))
                share = len(engines) // len(mine)
                tr["fwd"] = engines[k * share:(k + 1) * share]
        calls.append(transfers)
    return calls


def _helper(g, core, r, T, topo, cores, chips, groups, gid):
    sent = 0
    for call in _plan(r, cores, chips, groups, gid, topo):
        mine = [tr for tr in call if tr["via"] == core]
        if not mine:
            continue
        transfers = []
        for tr in mine:
            g.wait_ge(T.sem["rl%d" % tr["slot"]], len(tr["engines"]))
            rid, pid, _se = topo.addr(cores[tr["dst"]])
            s = tr["slot"]
            transfers.append(RemoteDMATransfer(dst_ids=[DstId(rid=rid, pnc=pid)], dma_engine_mask=_mask(tr["fwd"]),
                                               remote_sem=T.sem["ar%d" % r], src=T.relay[:, s * TK:(s + 1) * TK],
                                               dst=T.land[:, r * TK:(r + 1) * TK]))
            sent += len(tr["fwd"])
        g.remote_dma_fused(transfers, local_sem=T.sem.ls)
    if sent:
        g.wait_ge(T.sem.ls, sent)


def _incoming(r, j, cores, chips, groups, gid, topo):
    for call in _plan(j, cores, chips, groups, gid, topo):
        for tr in call:
            if tr["dst"] == r:
                return len(tr["engines"]) if tr["via"] is None else len(tr["fwd"])


def _runs(blocks):
    out = []
    for j in sorted(blocks):
        if out and out[-1][-1] + 1 == j:
            out[-1].append(j)
        else:
            out.append([j])
    return out


def rank_program(g, core, T, topo):
    cores, chips, groups, gid = _groups(T, topo)
    rank = T.rank_of(core)
    if rank is None:
        here = [r for r in range(len(cores)) if chips[r] == topo.chip(core)]
        if here:
            _helper(g, core, here[0], T, topo, cores, chips, groups, gid)
        return

    sem, te, ve = T.sem, g.tensor, g.vector
    calls = _plan(rank, cores, chips, groups, gid, topo)

    def to(kind, d):
        return _who(rank, kind, d, chips, groups, gid, topo)

    dma_of, n = {}, 0
    g.scalar.dma_start(T.f1s[:], T.f1[:]).then_inc(sem.sf1, 16)
    for k, piece in enumerate(LOADS):
        if k == len(LOADS) - 1:
            g.scalar.dma_start(T.f2s[:], T.f2[:]).then_inc(sem.sf2, 16)
        for run in _runs([to(kind, d) for kind, d in piece]):
            a, b = run[0] * TK, (run[-1] + 1) * TK
            g.sync.dma_start(T.xs[:, a:b], T.x[:, a:b]).then_inc(sem["sx%d" % n], 16)
            g.scalar.dma_start(T.ts[:, a:b], T.t[:, a:b]).then_inc(sem["st%d" % n], 16)
            for j in run:
                dma_of[j] = n
            n += 1

    done = {}
    reader = {}
    te.wait_ge(sem.sf1, 16)
    for i, unit in enumerate(UNITS):
        blocks = sorted(to(kind, d) for kind, d in unit)
        a, b = blocks[0] * TK, (blocks[-1] + 1) * TK
        bank = i % BANKS
        if bank in reader:
            te.wait_ge(sem[reader[bank]], 1)
        for k in sorted({dma_of[j] for j in blocks}):
            te.wait_ge(sem["sx%d" % k], 16)
        te.matmul(T["ps%d" % bank][:, 0:b - a], T.f1s[:], T.xs[:, a:b], start=True, stop=True).then_inc(sem["m1_%d" % i], 1)
        ve.wait_ge(sem["m1_%d" % i], 1)
        for k in sorted({dma_of[j] for j in blocks}):
            ve.wait_ge(sem["st%d" % k], 16)
        ve.tensor_tensor(out=T.us[:, a:b], in0=T["ps%d" % bank][:, 0:b - a], in1=T.ts[:, a:b],
                         op=AluOpType.mult).then_inc(sem["ud%d" % i], 1)
        reader[bank] = "ud%d" % i
        for j in blocks:
            done[j] = "ud%d" % i

    sent = 0
    for call in calls:
        for name in sorted({done[tr["dst"]] for tr in call}):
            g.wait_ge(sem[name], 1)
        transfers = []
        for tr in call:
            j = tr["dst"]
            if tr["via"] is None:
                target, out, arrived = cores[j], T.land[:, rank * TK:(rank + 1) * TK], sem["ar%d" % rank]
            else:
                target, out = tr["via"], T.relay[:, tr["slot"] * TK:(tr["slot"] + 1) * TK]
                arrived = sem["rl%d" % tr["slot"]]
            rid, pid, _se = topo.addr(target)
            transfers.append(RemoteDMATransfer(dst_ids=[DstId(rid=rid, pnc=pid)], dma_engine_mask=_mask(tr["engines"]),
                                               remote_sem=arrived, src=T.us[:, j * TK:(j + 1) * TK], dst=out))
            sent += len(tr["engines"])
        g.remote_dma_fused(transfers, local_sem=sem.ls)

    queues, stores = [g.sync, g.scalar], 0
    copied = {}
    te.wait_ge(sem.sf2, 16)
    for k, (kind, d) in enumerate(RECV):
        j = to(kind, -d)
        a, b = j * TK, (j + 1) * TK
        bank = (len(UNITS) + k) % BANKS
        if j == rank:
            te.wait_ge(sem[done[rank]], 1)
        else:
            te.wait_ge(sem["ar%d" % j], _incoming(rank, j, cores, chips, groups, gid, topo))
        te.wait_ge(sem[reader[bank]], 1)
        te.matmul(T["ps%d" % bank][:, 0:TK], T.f2s[:], T.us[:, a:b] if j == rank else T.land[:, a:b],
                  start=True, stop=True).then_inc(sem["m2_%d" % k], 1)
        ve.wait_ge(sem["m2_%d" % k], 1)
        ve.tensor_copy(T.ysb[:, a:b], T["ps%d" % bank][:, 0:TK]).then_inc(sem["cp%d" % k], 1)
        reader[bank] = "cp%d" % k
        copied[j] = "cp%d" % k
        members = [j] if d in SPLIT else groups[gid[j]]
        if all(m in copied for m in members):
            a, b = members[0] * TK, (members[-1] + 1) * TK
            qu = queues[stores % 2]
            for name in sorted({copied[m] for m in members}):
                qu.wait_ge(sem[name], 1)
            qu.dma_start(T.y[:, a:b], T.ysb[:, a:b]).then_inc(sem.yd, 16)
            stores += 1

    g.wait_ge(sem.ls, sent)
    g.wait_ge(sem.yd, 16 * stores)
